import numpy as np
import ml_dtypes


def mxq(x, axis, fmt="e4m3"):
    dtype, down = {"e4m3": (ml_dtypes.float8_e4m3fn, 7), "e5m2": (ml_dtypes.float8_e5m2, 14)}[fmt]
    v = np.moveaxis(np.asarray(x, np.float32).astype(ml_dtypes.bfloat16).astype(np.float64), axis, -1)
    blocks = v.reshape(v.shape[:-1] + (-1, 32))
    amax = np.abs(blocks).max(-1, keepdims=True)
    byte = np.maximum(np.where(amax > 0, np.frexp(amax)[1] - 1 + 127, 0) - down, 1)
    scale = np.exp2(byte - 127.0)
    codes = (blocks / scale).astype(np.float32).astype(dtype).astype(np.float64)
    return np.moveaxis((codes * scale).reshape(v.shape), -1, axis)


WIDE = False


def mx_kscale(k):
    if not WIDE:
        return np.ones(k)
    levels = np.array([24, -24, 12, -12, 0])
    if k % 512:
        return np.exp2(np.random.permutation(np.resize(levels, k // 32))).repeat(32)
    a = np.empty((k // 512, 16))
    for p in range(k // 512):
        a[p, :8] = np.random.permutation(np.resize(levels, 8))
        for g in range(8):
            far = levels[np.abs(levels - a[p, g]) >= 10]
            a[p, g + 8] = far[np.random.randint(len(far))]
    return np.exp2(a.ravel()).repeat(32)


def f64(x):
    return np.asarray(x).astype(np.float64)


def striped8(idx):
    return np.concatenate([v.reshape(-1, 16).T for v in idx]).astype(np.uint16)


def unstriped8(offs):
    return np.stack([offs[16 * g:16 * g + 16].T.reshape(-1) for g in range(8)]).astype(np.int64)


E2M1 = np.array([0.0, 0.5, 1.0, 1.5, 2.0, 3.0, 4.0, 6.0, -0.0, -0.5, -1.0, -1.5, -2.0, -3.0, -4.0, -6.0])


def pack_weight(w, fmt):
    k, n = w.shape
    w = f64(np.asarray(w, np.float32).astype(ml_dtypes.bfloat16)).reshape(k // 32, 32, n)
    amax = np.abs(w).max(1)
    if fmt == "e4m3":
        byte = np.frexp(amax)[1] - 1 + 127 - 7
    else:
        mant, ex = np.frexp(amax / 6.0)
        byte = np.where(mant > 0.5, ex, ex - 1) + 127
    byte = np.clip(np.where(amax > 0, byte, 1), 1, 254)
    scaled = (w * np.exp2(127.0 - byte)[:, None, :]).reshape(k, n).astype(np.float32)
    by_word = np.ascontiguousarray(scaled.reshape(k // 512, 128, 4, n).transpose(0, 1, 3, 2))
    if fmt == "e4m3":
        words = by_word.astype(ml_dtypes.float8_e4m3fn).view(np.uint8)
    else:
        c = by_word.astype(ml_dtypes.float4_e2m1fn).view(np.uint8) & 0xF
        words = (c[..., 0::2] | (c[..., 1::2] << 4)).reshape(k // 512, 128, 2 * n)
    return np.ascontiguousarray(words), np.ascontiguousarray(byte.astype(np.uint8).reshape(k // 512, 16, n))


def unpack_weight(words, scales, fmt):
    g, _, n = scales.shape
    words = np.ascontiguousarray(words).reshape(g, 128, n, -1)
    if fmt == "e4m3":
        vals = words.view(ml_dtypes.float8_e4m3fn).astype(np.float64)
    else:
        nib = np.empty((g, 128, n, 4), np.uint8)
        nib[..., 0::2] = words & 0xF
        nib[..., 1::2] = words >> 4
        vals = E2M1[nib]
    vals = vals * np.repeat(np.exp2(scales.astype(np.float64) - 127.0), 8, axis=1)[..., None]
    return vals.transpose(0, 1, 3, 2).reshape(g * 512, n)


def planes(y):
    n, m = y.shape
    v = y.astype(np.float32).astype(ml_dtypes.bfloat16).astype(np.float64).reshape(n // 32, 32, m)
    top = np.abs(v).max(1)
    byte = np.clip(np.where(top > 0, np.frexp(top)[1] - 1 + 127 - 7, 1), 1, 254)
    codes = (v * np.exp2(127.0 - byte)[:, None, :]).reshape(n, m).astype(np.float32).astype(ml_dtypes.float8_e4m3fn).view(np.uint8)
    words = codes.reshape(n // 512, 128, 4, m).transpose(0, 1, 3, 2)
    return np.ascontiguousarray(words), np.ascontiguousarray(byte.astype(np.uint8).reshape(n // 512, 16, m))


def silu(f):
    return f / (1.0 + np.exp(-np.maximum(f, -700.0)))


K, L, N, T, J = 512, 512, 512, 2048, 1024


def setup_inputs():
    n = np.random.standard_normal
    s = mx_kscale(K)[:, None]
    s2 = mx_kscale(L)[:, None]
    p_wa = pack_weight(n((K, N)) / np.sqrt(K) / s, "e2m1")
    return {
        "xT": (n((K, T)) * s).astype(np.float32),
        "wgt": np.repeat(np.random.uniform(0.5, 2.0, (8, J)), 16, axis=0).astype(np.float32),
        "zT": (n((L, T)) * s2).astype(np.float32),
        "wgt2": np.repeat(np.random.uniform(0.5, 2.0, (8, J)), 16, axis=0).astype(np.float32),
        "wa_words": p_wa[0],
        "wa_scales": p_wa[1],
        "wb": (n((L, N)) / np.sqrt(L) / s2).astype(np.float32),
        "b": (0.3 * n(N)).astype(np.float32),
        "offs": striped8(np.stack([np.random.permutation(T)[:J] for _ in range(8)])),
        "offs2": striped8(np.stack([np.random.permutation(T)[:J] for _ in range(8)])),
    }


def reference(xT, wgt, zT, wgt2, wa_words, wa_scales, wb, b, offs, offs2):
    idx = unstriped8(offs)
    idx2 = unstriped8(offs2)
    rows = np.arange(K)
    xg = f64(wgt)[rows // 4 % 128] * f64(xT)[rows[:, None], idx[rows % 512 // 64]]
    xT_ = mxq(xg, 0, "e4m3")
    rows = np.arange(L)
    xg = f64(wgt2)[rows // 4 % 128] * f64(zT)[rows[:, None], idx2[rows % 512 // 64]]
    zT_ = mxq(xg, 0, "e4m3")
    wa_ = unpack_weight(wa_words, wa_scales, "e2m1")
    wb_ = mxq(f64(wb), 0, "e4m3")
    ya = wa_.T @ xT_
    yb = wb_.T @ zT_
    out_0 = silu(np.abs(ya - yb) + f64(b)[:, None])
    return (out_0,) + planes(out_0)

@@ -1,0 +1,201 @@
+from contextlib import ExitStack
+
+import concourse.mybir as mybir
+
+K, L, N, T, J = 512, 512, 512, 2048, 1024
+FLOPS = 2 * K * N * J + 2 * L * N * J
+
+F32 = mybir.dt.float32
+BF16 = mybir.dt.bfloat16
+U32 = mybir.dt.uint32
+I32 = mybir.dt.int32
+U16 = mybir.dt.uint16
+U8 = mybir.dt.uint8
+FP8X4 = mybir.dt.float8_e4m3fn_x4
+FP4X4 = mybir.dt.float4_e2m1fn_x4
+ACT = mybir.ActivationFunctionType
+MULT = mybir.AluOpType.mult
+
+P = 128
+PACK = 4
+HALF = J // 2
+CHUNKS = ((0, 256), (256, 512), (768, 256))
+
+
+def weave(copy, grouped, planes, i0, i1):
+    copy(
+        out=grouped.rearrange("p (c e) i -> p c i e", e=4)[:, :, i0:i1, :],
+        in_=planes.rearrange("p i (c e) -> p c i e", e=4)[:, :, i0:i1, :],
+    )
+
+
+def quantize(nc, codes, scales, grouped):
+    nc.vector.quantize_mx(out=codes.bitcast(FP8X4), scales=scales, in_=grouped.rearrange("p j i -> p (j i)"))
+
+
+def tile_list_absd_siluP_kernel(
+    tc, xT, wgt, zT, wgt2, wa_words, wa_scales, wb, b, offs, offs2, out_0, out_1, out_2
+):
+    nc = tc.nc
+    with ExitStack() as ctx:
+        keep = ctx.enter_context(tc.tile_pool(name="keep", bufs=1))
+        psum = ctx.enter_context(tc.psum_pool(name="psum", bufs=1))
+
+        def sb(name, shape, dtype):
+            return keep.tile(shape, dtype, name=name, align_bytes=64)
+
+        x_list = sb("x_list", [P, J // 16], U16)
+        z_list = sb("z_list", [P, J // 16], U16)
+        x_planes = [sb("x_plane%d" % i, [P, T], F32) for i in range(PACK)]
+        z_planes = [sb("z_plane%d" % i, [P, T], F32) for i in range(PACK)]
+        x_wgt = [sb("x_wgt%d" % h, [P, HALF], F32) for h in range(2)]
+        z_wgt = sb("z_wgt", [P, J], F32)
+        wb_raw = sb("wb_raw", [P, PACK, N], F32)
+        wa_raw = sb("wa_raw", [P, 2 * N], U8)
+        wa_scales_raw = sb("wa_scales_raw", [P, N], U8)
+        bias = sb("bias", [P, PACK], F32)
+
+        x_rows = xT.rearrange("(p i) t -> p i t", i=PACK)
+        z_rows = zT.rearrange("(p i) t -> p i t", i=PACK)
+
+        nc.vector.memset(wa_scales_raw[:].bitcast(U32), 0)
+        for q in range(4):
+            nc.scalar.dma_start(
+                out=wa_scales_raw[32 * q : 32 * q + 4, :].bitcast(I32),
+                in_=wa_scales[0, 4 * q : 4 * q + 4, :].bitcast(I32),
+            )
+        nc.sync.dma_start(x_list[:], offs)
+        nc.sync.dma_start(out=wa_raw[:].bitcast(I32), in_=wa_words[0].bitcast(I32))
+        nc.sync.dma_start(out=x_wgt[0][:], in_=wgt[:, 0:HALF])
+        nc.sync.dma_start(out=x_planes[0][:], in_=x_rows[:, 0, :])
+        nc.sync.dma_start(out=x_wgt[1][:], in_=wgt[:, HALF:J])
+        for i in range(1, PACK):
+            nc.sync.dma_start(out=x_planes[i][:], in_=x_rows[:, i, :])
+        nc.sync.dma_start(z_list[:], offs2)
+        nc.sync.dma_start(out=bias[:], in_=b.rearrange("(p i) -> p i", i=PACK))
+        nc.sync.dma_start(out=z_wgt[:], in_=wgt2)
+        nc.sync.dma_start(out=z_planes[0][:], in_=z_rows[:, 0, :])
+        nc.sync.dma_start(out=wb_raw[:], in_=wb.rearrange("(p i) n -> p i n", i=PACK))
+        for i in range(1, PACK):
+            nc.sync.dma_start(out=z_planes[i][:], in_=z_rows[:, i, :])
+
+        wa_codes = sb("wa_codes", [P, 2 * N], U8)
+        wa_plane = sb("wa_plane", [P, N], U8)
+        nc.vector.tensor_copy(
+            out=wa_codes[:].rearrange("p (t m e) -> p t m e", t=PACK, e=2),
+            in_=wa_raw[:].rearrange("p (m t e) -> p t m e", t=PACK, e=2),
+        )
+        nc.vector.tensor_copy(
+            out=wa_plane[:].rearrange("p (t m) -> p t m", t=PACK),
+            in_=wa_scales_raw[:].rearrange("p (m t) -> p t m", t=PACK),
+        )
+
+        def gather(picked, plane, offsets, weights, j0, width):
+            nc.vector.tensor_tensor(
+                picked, plane[:].indirect(offsets[:, j0 // 16 : (j0 + width) // 16]), weights, MULT
+            )
+
+        xg = [sb("xg%d" % h, [P, PACK, HALF], F32) for h in range(2)]
+        xg_bf = [sb("xg_bf%d" % h, [P, HALF, PACK], BF16) for h in range(2)]
+        x_codes = sb("x_codes", [P, J], U32)
+        x_scales = sb("x_scales", [P, J], U8)
+        for i in range(PACK):
+            for h in range(2):
+                gather(xg[h][:, i, :], x_planes[i], x_list, x_wgt[h][:], h * HALF, HALF)
+        for h in range(2):
+            weave(nc.scalar.copy, xg_bf[h][:], xg[h][:], 0, PACK)
+
+        zg = [sb("zg%d" % c, [P, PACK, w], F32) for c, (j0, w) in enumerate(CHUNKS)]
+        zg_bf = [sb("zg_bf%d" % c, [P, w, PACK], BF16) for c, (j0, w) in enumerate(CHUNKS)]
+
+        def gather_z(i):
+            for c, (j0, w) in enumerate(CHUNKS):
+                gather(zg[c][:, i, :], z_planes[i], z_list, z_wgt[:, j0 : j0 + w], j0, w)
+
+        gather_z(0)
+        for h in range(2):
+            cols = slice(h * HALF, (h + 1) * HALF)
+            quantize(nc, x_codes[:, cols], x_scales[:, cols], xg_bf[h][:])
+
+        wb_bf = sb("wb_bf", [P, N, PACK], BF16)
+        wb_codes = sb("wb_codes", [P, N], U32)
+        wb_scales = sb("wb_scales", [P, N], U8)
+        nc.scalar.activation(
+            out=wb_bf[:].rearrange("p (t m) i -> p m t i", t=PACK),
+            in_=wb_raw[:].rearrange("p i (m t) -> p m t i", t=PACK),
+            func=ACT.Copy,
+            scale=-1.0,
+        )
+        gather_z(1)
+        quantize(nc, wb_codes[:], wb_scales[:], wb_bf[:])
+        for c in range(len(CHUNKS)):
+            weave(nc.scalar.copy, zg_bf[c][:], zg[c][:], 0, 2)
+        gather_z(2)
+
+        banks = [psum.tile([P, 512], F32, name="bank%d" % n) for n in range(2 * PACK)]
+
+        def acc(c, t):
+            if c == 1:
+                return banks[PACK + t][:]
+            return banks[t][:, 0:256] if c == 0 else banks[t][:, 256:512]
+
+        def x_passes(c):
+            j0, w = CHUNKS[c]
+            step = 512 if w == 512 else 128
+            for t in range(PACK):
+                for s in range(0, w, step):
+                    nc.tensor.matmul_mx(
+                        out=acc(c, t)[:, s : s + step],
+                        lhsT=wa_codes[:, 256 * t : 256 * (t + 1)].bitcast(FP4X4),
+                        lhsT_scale=wa_plane[:, P * t : P * (t + 1)],
+                        rhs=x_codes[:, j0 + s : j0 + s + step].bitcast(FP8X4),
+                        rhs_scale=x_scales[:, j0 + s : j0 + s + step],
+                        start=(s == 0),
+                        stop=False,
+                    )
+
+        x_passes(0)
+        x_passes(1)
+
+        z_codes = [sb("z_codes%d" % c, [P, w], U32) for c, (j0, w) in enumerate(CHUNKS)]
+        z_scales = [sb("z_scales%d" % c, [P, w], U8) for c, (j0, w) in enumerate(CHUNKS)]
+        for c, (j0, w) in enumerate(CHUNKS):
+            gather(zg[c][:, 3, :], z_planes[3], z_list, z_wgt[:, j0 : j0 + w], j0, w)
+            weave(nc.vector.tensor_copy, zg_bf[c][:], zg[c][:], 2, PACK)
+            quantize(nc, z_codes[c][:], z_scales[c][:], zg_bf[c][:])
+
+        out_rows = out_0.rearrange("(p t) j -> p t j", t=PACK)
+        out_words = out_1[0].rearrange("p j i -> p (j i)").bitcast(I32)
+        y_codes = sb("y_codes", [P, J], U32)
+        y_scales = sb("y_scales", [P, J], U8)
+        for c, (j0, w) in enumerate(CHUNKS):
+            dist = sb("dist%d" % c, [P, PACK, w], F32)
+            y = sb("y%d" % c, [P, PACK, w], F32)
+            y_bf = sb("y_bf%d" % c, [P, w, PACK], BF16)
+            if c == 2:
+                x_passes(2)
+            for t in range(PACK):
+                nc.tensor.matmul_mx(
+                    out=acc(c, t),
+                    lhsT=wb_codes[:, P * t : P * (t + 1)].bitcast(FP8X4),
+                    lhsT_scale=wb_scales[:, P * t : P * (t + 1)],
+                    rhs=z_codes[c][:].bitcast(FP8X4),
+                    rhs_scale=z_scales[c][:],
+                    start=False,
+                    stop=True,
+                )
+            for t in range(PACK):
+                nc.scalar.activation(out=dist[:, t, :], in_=acc(c, t), func=ACT.Abs)
+                nc.scalar.activation(out=y[:, t, :], in_=dist[:, t, :], func=ACT.Silu, bias=bias[:, t : t + 1])
+                nc.sync.dma_start(out=out_rows[:, t, j0 : j0 + w], in_=y[:, t, :])
+            weave(nc.vector.tensor_copy, y_bf[:], y[:], 0, PACK)
+            quantize(nc, y_codes[:, j0 : j0 + w], y_scales[:, j0 : j0 + w], y_bf[:])
+            nc.sync.dma_start(out=out_words[:, j0 : j0 + w], in_=y_codes[:, j0 : j0 + w].bitcast(I32))
+            if c >= 1:
+                cols = slice(0, 768) if c == 1 else slice(768, J)
+                for q in range(4):
+                    queue = nc.scalar if c == 2 and q % 2 else nc.sync
+                    queue.dma_start(
+                        out=out_2[0, 4 * q : 4 * q + 4, cols].bitcast(I32),
+                        in_=y_scales[32 * q : 32 * q + 4, cols].bitcast(I32),
+                    )

@@ -1,6 +1,7 @@
 from contextlib import ExitStack
 
 import concourse.mybir as mybir
+from concourse.masks import make_identity
 
 K, L, N, T, J = 512, 512, 512, 2048, 1024
 FLOPS = 2 * K * N * J + 2 * L * N * J
@@ -19,13 +20,14 @@ MULT = mybir.AluOpType.mult
 P = 128
 PACK = 4
 HALF = J // 2
-CHUNKS = ((0, 256), (256, 512), (768, 256))
+W = 256
+CHUNKS = ((0, 128), (128, 256), (384, 256), (640, 256), (896, 128))
 
 
-def weave(copy, grouped, planes, i0, i1):
+def weave(copy, grouped, planes):
     copy(
-        out=grouped.rearrange("p (c e) i -> p c i e", e=4)[:, :, i0:i1, :],
-        in_=planes.rearrange("p i (c e) -> p c i e", e=4)[:, :, i0:i1, :],
+        out=grouped.rearrange("p (c e) i -> p c i e", e=4),
+        in_=planes.rearrange("p i (c e) -> p c i e", e=4),
     )
 
 
@@ -41,14 +43,14 @@ def tile_list_absd_siluP_kernel(
         keep = ctx.enter_context(tc.tile_pool(name="keep", bufs=1))
         psum = ctx.enter_context(tc.psum_pool(name="psum", bufs=1))
 
-        def sb(name, shape, dtype):
-            return keep.tile(shape, dtype, name=name, align_bytes=64)
+        def sb(name, shape, dtype, tag=None):
+            return keep.tile(shape, dtype, name=name, tag=tag or name, align_bytes=64)
 
         x_list = sb("x_list", [P, J // 16], U16)
         z_list = sb("z_list", [P, J // 16], U16)
         x_planes = [sb("x_plane%d" % i, [P, T], F32) for i in range(PACK)]
         z_planes = [sb("z_plane%d" % i, [P, T], F32) for i in range(PACK)]
-        x_wgt = [sb("x_wgt%d" % h, [P, HALF], F32) for h in range(2)]
+        x_wgt = sb("x_wgt", [P, J], F32)
         z_wgt = sb("z_wgt", [P, J], F32)
         wb_raw = sb("wb_raw", [P, PACK, N], F32)
         wa_raw = sb("wa_raw", [P, 2 * N], U8)
@@ -58,67 +60,97 @@ def tile_list_absd_siluP_kernel(
         x_rows = xT.rearrange("(p i) t -> p i t", i=PACK)
         z_rows = zT.rearrange("(p i) t -> p i t", i=PACK)
 
+        warm = sb("warm", [P, 2], F32)
+        nc.vector.memset(warm[:, 0:1], 0.0)
+        wgt_rows = sb("wgt_rows", [P, HALF], F32)
+        nc.vector.memset(wgt_rows[64:P, :], 0.0)
         nc.vector.memset(wa_scales_raw[:].bitcast(U32), 0)
-        for q in range(4):
-            nc.scalar.dma_start(
+        identity = sb("identity", [P, P], F32)
+        make_identity(nc, identity[:])
+        nc.scalar.activation(out=warm[:, 1:2], in_=warm[:, 0:1], func=ACT.Silu)
+
+        def load_scale_rows(q):
+            nc.sync.dma_start(
                 out=wa_scales_raw[32 * q : 32 * q + 4, :].bitcast(I32),
                 in_=wa_scales[0, 4 * q : 4 * q + 4, :].bitcast(I32),
             )
+
+        halves = ((wgt, x_wgt, HALF, 0, 16), (wgt2, z_wgt, 0, 16, 16), (wgt2, z_wgt, HALF, 32, 32))
+        for source, weights, j0, first, rows in halves:
+            nc.sync.dma_start(out=wgt_rows[first : first + rows, :], in_=source[0 : P : P // rows, j0 : j0 + HALF])
         nc.sync.dma_start(x_list[:], offs)
         nc.sync.dma_start(out=wa_raw[:].bitcast(I32), in_=wa_words[0].bitcast(I32))
-        nc.sync.dma_start(out=x_wgt[0][:], in_=wgt[:, 0:HALF])
+        nc.sync.dma_start(out=x_wgt[:, 0:HALF], in_=wgt[:, 0:HALF])
         nc.sync.dma_start(out=x_planes[0][:], in_=x_rows[:, 0, :])
-        nc.sync.dma_start(out=x_wgt[1][:], in_=wgt[:, HALF:J])
         for i in range(1, PACK):
             nc.sync.dma_start(out=x_planes[i][:], in_=x_rows[:, i, :])
-        nc.sync.dma_start(z_list[:], offs2)
-        nc.sync.dma_start(out=bias[:], in_=b.rearrange("(p i) -> p i", i=PACK))
-        nc.sync.dma_start(out=z_wgt[:], in_=wgt2)
+        for q in range(4):
+            load_scale_rows(q)
         nc.sync.dma_start(out=z_planes[0][:], in_=z_rows[:, 0, :])
+        nc.sync.dma_start(z_list[:], offs2)
         nc.sync.dma_start(out=wb_raw[:], in_=wb.rearrange("(p i) n -> p i n", i=PACK))
-        for i in range(1, PACK):
-            nc.sync.dma_start(out=z_planes[i][:], in_=z_rows[:, i, :])
+        nc.sync.dma_start(out=z_planes[1][:], in_=z_rows[:, 1, :])
+        nc.sync.dma_start(out=z_planes[2][:], in_=z_rows[:, 2, :])
+        nc.sync.dma_start(out=bias[:], in_=b.rearrange("(p i) -> p i", i=PACK))
+        nc.sync.dma_start(out=z_planes[3][:], in_=z_rows[:, 3, :])
+
+        banks = [psum.tile([P, 2 * W], F32, name="bank%d" % n) for n in range(2 * PACK)]
+        for jb in range(4):
+            nc.tensor.transpose(banks[0][:, jb * P : (jb + 1) * P], wgt_rows[:, jb * P : (jb + 1) * P], identity[:])
+        for n, (source, weights, j0, first, rows) in enumerate(halves):
+            spread = sb("spread%d" % n, [P, HALF], F32, tag="spread")
+            columns = banks[0][:].rearrange("p (b u) -> p b u", b=4)[:, :, first : first + rows]
+            nc.scalar.copy(
+                out=spread[:].rearrange("p (b u r) -> p b u r", b=4, u=rows),
+                in_=columns.unsqueeze(3).to_broadcast([P, 4, rows, P // rows]),
+            )
+            for jb in range(4):
+                nc.tensor.transpose(
+                    banks[1 + n][:, jb * P : (jb + 1) * P], spread[:, jb * P : (jb + 1) * P], identity[:]
+                )
+            nc.scalar.copy(out=weights[:, j0 : j0 + HALF], in_=banks[1 + n][:])
 
         wa_codes = sb("wa_codes", [P, 2 * N], U8)
-        wa_plane = sb("wa_plane", [P, N], U8)
         nc.vector.tensor_copy(
             out=wa_codes[:].rearrange("p (t m e) -> p t m e", t=PACK, e=2),
             in_=wa_raw[:].rearrange("p (m t e) -> p t m e", t=PACK, e=2),
         )
+
+        def gather(picked, plane, offsets, weights, j0, width):
+            nc.vector.tensor_tensor(
+                picked,
+                plane[:].indirect(offsets[:, j0 // 16 : (j0 + width) // 16]),
+                weights[:, j0 : j0 + width],
+                MULT,
+            )
+
+        xg = [sb("xg%d" % u, [P, 2, J], F32) for u in range(2)]
+        xg_bf = [sb("xg_bf%d" % h, [P, HALF, PACK], BF16) for h in range(2)]
+        for i in range(PACK):
+            width = HALF if i in (0, PACK - 1) else J
+            for j0 in range(0, J, width):
+                gather(xg[i // 2][:, i % 2, j0 : j0 + width], x_planes[i], x_list, x_wgt, j0, width)
+            if i % 2:
+                for h in range(2):
+                    weave(nc.scalar.copy, xg_bf[h][:, :, i - 1 : i + 1], xg[i // 2][:, :, h * HALF : (h + 1) * HALF])
+
+        wa_plane = sb("wa_plane", [P, N], U8, tag="x_plane3")
         nc.vector.tensor_copy(
             out=wa_plane[:].rearrange("p (t m) -> p t m", t=PACK),
             in_=wa_scales_raw[:].rearrange("p (m t) -> p t m", t=PACK),
         )
 
-        def gather(picked, plane, offsets, weights, j0, width):
-            nc.vector.tensor_tensor(
-                picked, plane[:].indirect(offsets[:, j0 // 16 : (j0 + width) // 16]), weights, MULT
-            )
-
-        xg = [sb("xg%d" % h, [P, PACK, HALF], F32) for h in range(2)]
-        xg_bf = [sb("xg_bf%d" % h, [P, HALF, PACK], BF16) for h in range(2)]
-        x_codes = sb("x_codes", [P, J], U32)
-        x_scales = sb("x_scales", [P, J], U8)
-        for i in range(PACK):
-            for h in range(2):
-                gather(xg[h][:, i, :], x_planes[i], x_list, x_wgt[h][:], h * HALF, HALF)
-        for h in range(2):
-            weave(nc.scalar.copy, xg_bf[h][:], xg[h][:], 0, PACK)
-
-        zg = [sb("zg%d" % c, [P, PACK, w], F32) for c, (j0, w) in enumerate(CHUNKS)]
+        zg_lo = sb("zg_lo", [P, 2, J], F32)
         zg_bf = [sb("zg_bf%d" % c, [P, w, PACK], BF16) for c, (j0, w) in enumerate(CHUNKS)]
-
-        def gather_z(i):
-            for c, (j0, w) in enumerate(CHUNKS):
-                gather(zg[c][:, i, :], z_planes[i], z_list, z_wgt[:, j0 : j0 + w], j0, w)
-
-        gather_z(0)
+        gather(zg_lo[:, 0, :], z_planes[0], z_list, z_wgt, 0, J)
+        x_codes = [sb("x_codes0", [P, HALF], U32, tag="z_plane0")[:]]
+        x_scales = sb("x_scales", [P, J], U8)
+        quantize(nc, x_codes[0], x_scales[:, 0:HALF], xg_bf[0][:])
         for h in range(2):
-            cols = slice(h * HALF, (h + 1) * HALF)
-            quantize(nc, x_codes[:, cols], x_scales[:, cols], xg_bf[h][:])
+            gather(zg_lo[:, 1, h * HALF : (h + 1) * HALF], z_planes[1], z_list, z_wgt, h * HALF, HALF)
 
         wb_bf = sb("wb_bf", [P, N, PACK], BF16)
-        wb_codes = sb("wb_codes", [P, N], U32)
+        wb_codes = sb("wb_codes", [P, N], U32, tag="z_plane1")[:]
         wb_scales = sb("wb_scales", [P, N], U8)
         nc.scalar.activation(
             out=wb_bf[:].rearrange("p (t m) i -> p m t i", t=PACK),
@@ -126,55 +158,58 @@ def tile_list_absd_siluP_kernel(
             func=ACT.Copy,
             scale=-1.0,
         )
-        gather_z(1)
-        quantize(nc, wb_codes[:], wb_scales[:], wb_bf[:])
-        for c in range(len(CHUNKS)):
-            weave(nc.scalar.copy, zg_bf[c][:], zg[c][:], 0, 2)
-        gather_z(2)
+        for c, (j0, w) in enumerate(CHUNKS):
+            weave(nc.scalar.copy, zg_bf[c][:, :, 0:2], zg_lo[:, :, j0 : j0 + w])
+        quantize(nc, wb_codes, wb_scales[:], wb_bf[:])
 
-        banks = [psum.tile([P, 512], F32, name="bank%d" % n) for n in range(2 * PACK)]
 
         def acc(c, t):
-            if c == 1:
-                return banks[PACK + t][:]
-            return banks[t][:, 0:256] if c == 0 else banks[t][:, 256:512]
+            used = sum(w for j0, w in CHUNKS[c % 2 : c : 2])
+            return banks[PACK * (c % 2) + t][:, used : used + CHUNKS[c][1]]
 
-        def x_passes(c):
+        def x_passes(c, t):
             j0, w = CHUNKS[c]
-            step = 512 if w == 512 else 128
-            for t in range(PACK):
-                for s in range(0, w, step):
-                    nc.tensor.matmul_mx(
-                        out=acc(c, t)[:, s : s + step],
-                        lhsT=wa_codes[:, 256 * t : 256 * (t + 1)].bitcast(FP4X4),
-                        lhsT_scale=wa_plane[:, P * t : P * (t + 1)],
-                        rhs=x_codes[:, j0 + s : j0 + s + step].bitcast(FP8X4),
-                        rhs_scale=x_scales[:, j0 + s : j0 + s + step],
-                        start=(s == 0),
-                        stop=False,
-                    )
+            for s in range(0, w, P):
+                j = j0 + s
+                nc.tensor.matmul_mx(
+                    out=acc(c, t)[:, s : s + P],
+                    lhsT=wa_codes[:, 256 * t : 256 * (t + 1)].bitcast(FP4X4),
+                    lhsT_scale=wa_plane[:, P * t : P * (t + 1)],
+                    rhs=x_codes[j // HALF][:, j % HALF : j % HALF + P].bitcast(FP8X4),
+                    rhs_scale=x_scales[:, j : j + P],
+                    start=(s == 0),
+                    stop=False,
+                )
 
-        x_passes(0)
-        x_passes(1)
+        for c in range(2):
+            for t in range(PACK):
+                x_passes(c, t)
 
         z_codes = [sb("z_codes%d" % c, [P, w], U32) for c, (j0, w) in enumerate(CHUNKS)]
         z_scales = [sb("z_scales%d" % c, [P, w], U8) for c, (j0, w) in enumerate(CHUNKS)]
         for c, (j0, w) in enumerate(CHUNKS):
-            gather(zg[c][:, 3, :], z_planes[3], z_list, z_wgt[:, j0 : j0 + w], j0, w)
-            weave(nc.vector.tensor_copy, zg_bf[c][:], zg[c][:], 2, PACK)
+            zg_hi = sb("zg_hi%d" % c, [P, 2, w], F32, tag="zg_hi%d" % (c % 2))
+            for i in range(2):
+                gather(zg_hi[:, i, :], z_planes[2 + i], z_list, z_wgt, j0, w)
+            weave(nc.scalar.copy if c < 2 else nc.vector.tensor_copy, zg_bf[c][:, :, 2:4], zg_hi[:])
             quantize(nc, z_codes[c][:], z_scales[c][:], zg_bf[c][:])
+            if c == 1:
+                x_codes.append(sb("x_codes1", [P, HALF], U32, tag="zg_bf0")[:])
+                quantize(nc, x_codes[1], x_scales[:, HALF:J], xg_bf[1][:])
 
         out_rows = out_0.rearrange("(p t) j -> p t j", t=PACK)
         out_words = out_1[0].rearrange("p j i -> p (j i)").bitcast(I32)
         y_codes = sb("y_codes", [P, J], U32)
         y_scales = sb("y_scales", [P, J], U8)
         for c, (j0, w) in enumerate(CHUNKS):
+            cols = slice(j0, j0 + w)
+            last = c == len(CHUNKS) - 1
             dist = sb("dist%d" % c, [P, PACK, w], F32)
             y = sb("y%d" % c, [P, PACK, w], F32)
-            y_bf = sb("y_bf%d" % c, [P, w, PACK], BF16)
-            if c == 2:
-                x_passes(2)
+            y_bf = sb("y_bf%d" % c, [P, w, PACK], BF16, tag="zg_bf%d" % (len(CHUNKS) - 1 - c))
             for t in range(PACK):
+                if c >= 2:
+                    x_passes(c, t)
                 nc.tensor.matmul_mx(
                     out=acc(c, t),
                     lhsT=wb_codes[:, P * t : P * (t + 1)].bitcast(FP8X4),
@@ -187,15 +222,20 @@ def tile_list_absd_siluP_kernel(
             for t in range(PACK):
                 nc.scalar.activation(out=dist[:, t, :], in_=acc(c, t), func=ACT.Abs)
                 nc.scalar.activation(out=y[:, t, :], in_=dist[:, t, :], func=ACT.Silu, bias=bias[:, t : t + 1])
-                nc.sync.dma_start(out=out_rows[:, t, j0 : j0 + w], in_=y[:, t, :])
-            weave(nc.vector.tensor_copy, y_bf[:], y[:], 0, PACK)
-            quantize(nc, y_codes[:, j0 : j0 + w], y_scales[:, j0 : j0 + w], y_bf[:])
-            nc.sync.dma_start(out=out_words[:, j0 : j0 + w], in_=y_codes[:, j0 : j0 + w].bitcast(I32))
-            if c >= 1:
-                cols = slice(0, 768) if c == 1 else slice(768, J)
-                for q in range(4):
-                    queue = nc.scalar if c == 2 and q % 2 else nc.sync
-                    queue.dma_start(
-                        out=out_2[0, 4 * q : 4 * q + 4, cols].bitcast(I32),
-                        in_=y_scales[32 * q : 32 * q + 4, cols].bitcast(I32),
-                    )
+                if t % 2:
+                    rows = slice(t - 1, t + 1)
+                    nc.sync.dma_start(out=out_rows[:, rows, cols], in_=y[:, rows, :])
+                if last and t % 2:
+                    weave(nc.vector.tensor_copy, y_bf[:, :, t - 1 : t + 1], y[:, t - 1 : t + 1, :])
+            if not last:
+                weave(nc.vector.tensor_copy, y_bf[:], y[:])
+            quantize(nc, y_codes[:, cols], y_scales[:, cols], y_bf[:])
+            if c >= 2:
+                done = slice(0, j0 + w) if c == 2 else cols
+                nc.sync.dma_start(out=out_words[:, done], in_=y_codes[:, done].bitcast(I32))
+        for q in range(4):
+            queue = nc.scalar if q % 2 else nc.sync
+            queue.dma_start(
+                out=out_2[0, 4 * q : 4 * q + 4, :].bitcast(I32),
+                in_=y_scales[32 * q : 32 * q + 4, :].bitcast(I32),
+            )

from contextlib import ExitStack

import concourse.mybir as mybir
from concourse.masks import make_identity

K, L, N, T, J = 512, 512, 512, 2048, 1024
FLOPS = 2 * K * N * J + 2 * L * N * J

F32 = mybir.dt.float32
BF16 = mybir.dt.bfloat16
U32 = mybir.dt.uint32
I32 = mybir.dt.int32
U16 = mybir.dt.uint16
U8 = mybir.dt.uint8
FP8X4 = mybir.dt.float8_e4m3fn_x4
FP4X4 = mybir.dt.float4_e2m1fn_x4
ACT = mybir.ActivationFunctionType
MULT = mybir.AluOpType.mult

P = 128
PACK = 4
HALF = J // 2
W = 256
CHUNKS = ((0, 128), (128, 256), (384, 256), (640, 256), (896, 128))


def weave(copy, grouped, planes):
    copy(
        out=grouped.rearrange("p (c e) i -> p c i e", e=4),
        in_=planes.rearrange("p i (c e) -> p c i e", e=4),
    )


def quantize(nc, codes, scales, grouped):
    nc.vector.quantize_mx(out=codes.bitcast(FP8X4), scales=scales, in_=grouped.rearrange("p j i -> p (j i)"))


def tile_list_absd_siluP_kernel(
    tc, xT, wgt, zT, wgt2, wa_words, wa_scales, wb, b, offs, offs2, out_0, out_1, out_2
):
    nc = tc.nc
    with ExitStack() as ctx:
        keep = ctx.enter_context(tc.tile_pool(name="keep", bufs=1))
        psum = ctx.enter_context(tc.psum_pool(name="psum", bufs=1))

        def sb(name, shape, dtype, tag=None):
            return keep.tile(shape, dtype, name=name, tag=tag or name, align_bytes=64)

        x_list = sb("x_list", [P, J // 16], U16)
        z_list = sb("z_list", [P, J // 16], U16)
        x_planes = [sb("x_plane%d" % i, [P, T], F32) for i in range(PACK)]
        z_planes = [sb("z_plane%d" % i, [P, T], F32) for i in range(PACK)]
        x_wgt = sb("x_wgt", [P, J], F32)
        z_wgt = sb("z_wgt", [P, J], F32)
        wb_raw = sb("wb_raw", [P, PACK, N], F32)
        wa_raw = sb("wa_raw", [P, 2 * N], U8)
        wa_scales_raw = sb("wa_scales_raw", [P, N], U8)
        bias = sb("bias", [P, PACK], F32)

        x_rows = xT.rearrange("(p i) t -> p i t", i=PACK)
        z_rows = zT.rearrange("(p i) t -> p i t", i=PACK)

        warm = sb("warm", [P, 2], F32)
        nc.vector.memset(warm[:, 0:1], 0.0)
        wgt_rows = sb("wgt_rows", [P, HALF], F32)
        nc.vector.memset(wgt_rows[64:P, :], 0.0)
        nc.vector.memset(wa_scales_raw[:].bitcast(U32), 0)
        identity = sb("identity", [P, P], F32)
        make_identity(nc, identity[:])
        nc.scalar.activation(out=warm[:, 1:2], in_=warm[:, 0:1], func=ACT.Silu)

        def load_scale_rows(q):
            nc.sync.dma_start(
                out=wa_scales_raw[32 * q : 32 * q + 4, :].bitcast(I32),
                in_=wa_scales[0, 4 * q : 4 * q + 4, :].bitcast(I32),
            )

        halves = ((wgt, x_wgt, HALF, 0, 16), (wgt2, z_wgt, 0, 16, 16), (wgt2, z_wgt, HALF, 32, 32))
        for source, weights, j0, first, rows in halves:
            nc.sync.dma_start(out=wgt_rows[first : first + rows, :], in_=source[0 : P : P // rows, j0 : j0 + HALF])
        nc.sync.dma_start(x_list[:], offs)
        nc.sync.dma_start(out=wa_raw[:].bitcast(I32), in_=wa_words[0].bitcast(I32))
        nc.sync.dma_start(out=x_wgt[:, 0:HALF], in_=wgt[:, 0:HALF])
        nc.sync.dma_start(out=x_planes[0][:], in_=x_rows[:, 0, :])
        for i in range(1, PACK):
            nc.sync.dma_start(out=x_planes[i][:], in_=x_rows[:, i, :])
        for q in range(4):
            load_scale_rows(q)
        nc.sync.dma_start(out=z_planes[0][:], in_=z_rows[:, 0, :])
        nc.sync.dma_start(z_list[:], offs2)
        nc.sync.dma_start(out=wb_raw[:], in_=wb.rearrange("(p i) n -> p i n", i=PACK))
        nc.sync.dma_start(out=z_planes[1][:], in_=z_rows[:, 1, :])
        nc.sync.dma_start(out=z_planes[2][:], in_=z_rows[:, 2, :])
        nc.sync.dma_start(out=bias[:], in_=b.rearrange("(p i) -> p i", i=PACK))
        nc.sync.dma_start(out=z_planes[3][:], in_=z_rows[:, 3, :])

        banks = [psum.tile([P, 2 * W], F32, name="bank%d" % n) for n in range(2 * PACK)]
        for jb in range(4):
            nc.tensor.transpose(banks[0][:, jb * P : (jb + 1) * P], wgt_rows[:, jb * P : (jb + 1) * P], identity[:])
        for n, (source, weights, j0, first, rows) in enumerate(halves):
            spread = sb("spread%d" % n, [P, HALF], F32, tag="spread")
            columns = banks[0][:].rearrange("p (b u) -> p b u", b=4)[:, :, first : first + rows]
            nc.scalar.copy(
                out=spread[:].rearrange("p (b u r) -> p b u r", b=4, u=rows),
                in_=columns.unsqueeze(3).to_broadcast([P, 4, rows, P // rows]),
            )
            for jb in range(4):
                nc.tensor.transpose(
                    banks[1 + n][:, jb * P : (jb + 1) * P], spread[:, jb * P : (jb + 1) * P], identity[:]
                )
            nc.scalar.copy(out=weights[:, j0 : j0 + HALF], in_=banks[1 + n][:])

        wa_codes = sb("wa_codes", [P, 2 * N], U8)
        nc.vector.tensor_copy(
            out=wa_codes[:].rearrange("p (t m e) -> p t m e", t=PACK, e=2),
            in_=wa_raw[:].rearrange("p (m t e) -> p t m e", t=PACK, e=2),
        )

        def gather(picked, plane, offsets, weights, j0, width):
            nc.vector.tensor_tensor(
                picked,
                plane[:].indirect(offsets[:, j0 // 16 : (j0 + width) // 16]),
                weights[:, j0 : j0 + width],
                MULT,
            )

        xg = [sb("xg%d" % u, [P, 2, J], F32) for u in range(2)]
        xg_bf = [sb("xg_bf%d" % h, [P, HALF, PACK], BF16) for h in range(2)]
        for i in range(PACK):
            width = HALF if i in (0, PACK - 1) else J
            for j0 in range(0, J, width):
                gather(xg[i // 2][:, i % 2, j0 : j0 + width], x_planes[i], x_list, x_wgt, j0, width)
            if i % 2:
                for h in range(2):
                    weave(nc.scalar.copy, xg_bf[h][:, :, i - 1 : i + 1], xg[i // 2][:, :, h * HALF : (h + 1) * HALF])

        wa_plane = sb("wa_plane", [P, N], U8, tag="x_plane3")
        nc.vector.tensor_copy(
            out=wa_plane[:].rearrange("p (t m) -> p t m", t=PACK),
            in_=wa_scales_raw[:].rearrange("p (m t) -> p t m", t=PACK),
        )

        zg_lo = sb("zg_lo", [P, 2, J], F32)
        zg_bf = [sb("zg_bf%d" % c, [P, w, PACK], BF16) for c, (j0, w) in enumerate(CHUNKS)]
        gather(zg_lo[:, 0, :], z_planes[0], z_list, z_wgt, 0, J)
        x_codes = [sb("x_codes0", [P, HALF], U32, tag="z_plane0")[:]]
        x_scales = sb("x_scales", [P, J], U8)
        quantize(nc, x_codes[0], x_scales[:, 0:HALF], xg_bf[0][:])
        for h in range(2):
            gather(zg_lo[:, 1, h * HALF : (h + 1) * HALF], z_planes[1], z_list, z_wgt, h * HALF, HALF)

        wb_bf = sb("wb_bf", [P, N, PACK], BF16)
        wb_codes = sb("wb_codes", [P, N], U32, tag="z_plane1")[:]
        wb_scales = sb("wb_scales", [P, N], U8)
        nc.scalar.activation(
            out=wb_bf[:].rearrange("p (t m) i -> p m t i", t=PACK),
            in_=wb_raw[:].rearrange("p i (m t) -> p m t i", t=PACK),
            func=ACT.Copy,
            scale=-1.0,
        )
        for c, (j0, w) in enumerate(CHUNKS):
            weave(nc.scalar.copy, zg_bf[c][:, :, 0:2], zg_lo[:, :, j0 : j0 + w])
        quantize(nc, wb_codes, wb_scales[:], wb_bf[:])


        def acc(c, t):
            used = sum(w for j0, w in CHUNKS[c % 2 : c : 2])
            return banks[PACK * (c % 2) + t][:, used : used + CHUNKS[c][1]]

        def x_passes(c, t):
            j0, w = CHUNKS[c]
            for s in range(0, w, P):
                j = j0 + s
                nc.tensor.matmul_mx(
                    out=acc(c, t)[:, s : s + P],
                    lhsT=wa_codes[:, 256 * t : 256 * (t + 1)].bitcast(FP4X4),
                    lhsT_scale=wa_plane[:, P * t : P * (t + 1)],
                    rhs=x_codes[j // HALF][:, j % HALF : j % HALF + P].bitcast(FP8X4),
                    rhs_scale=x_scales[:, j : j + P],
                    start=(s == 0),
                    stop=False,
                )

        for c in range(2):
            for t in range(PACK):
                x_passes(c, t)

        z_codes = [sb("z_codes%d" % c, [P, w], U32) for c, (j0, w) in enumerate(CHUNKS)]
        z_scales = [sb("z_scales%d" % c, [P, w], U8) for c, (j0, w) in enumerate(CHUNKS)]
        for c, (j0, w) in enumerate(CHUNKS):
            zg_hi = sb("zg_hi%d" % c, [P, 2, w], F32, tag="zg_hi%d" % (c % 2))
            for i in range(2):
                gather(zg_hi[:, i, :], z_planes[2 + i], z_list, z_wgt, j0, w)
            weave(nc.scalar.copy if c < 2 else nc.vector.tensor_copy, zg_bf[c][:, :, 2:4], zg_hi[:])
            quantize(nc, z_codes[c][:], z_scales[c][:], zg_bf[c][:])
            if c == 1:
                x_codes.append(sb("x_codes1", [P, HALF], U32, tag="zg_bf0")[:])
                quantize(nc, x_codes[1], x_scales[:, HALF:J], xg_bf[1][:])

        out_rows = out_0.rearrange("(p t) j -> p t j", t=PACK)
        out_words = out_1[0].rearrange("p j i -> p (j i)").bitcast(I32)
        y_codes = sb("y_codes", [P, J], U32)
        y_scales = sb("y_scales", [P, J], U8)
        for c, (j0, w) in enumerate(CHUNKS):
            cols = slice(j0, j0 + w)
            last = c == len(CHUNKS) - 1
            dist = sb("dist%d" % c, [P, PACK, w], F32)
            y = sb("y%d" % c, [P, PACK, w], F32)
            y_bf = sb("y_bf%d" % c, [P, w, PACK], BF16, tag="zg_bf%d" % (len(CHUNKS) - 1 - c))
            for t in range(PACK):
                if c >= 2:
                    x_passes(c, t)
                nc.tensor.matmul_mx(
                    out=acc(c, t),
                    lhsT=wb_codes[:, P * t : P * (t + 1)].bitcast(FP8X4),
                    lhsT_scale=wb_scales[:, P * t : P * (t + 1)],
                    rhs=z_codes[c][:].bitcast(FP8X4),
                    rhs_scale=z_scales[c][:],
                    start=False,
                    stop=True,
                )
            for t in range(PACK):
                nc.scalar.activation(out=dist[:, t, :], in_=acc(c, t), func=ACT.Abs)
                nc.scalar.activation(out=y[:, t, :], in_=dist[:, t, :], func=ACT.Silu, bias=bias[:, t : t + 1])
                if t % 2:
                    rows = slice(t - 1, t + 1)
                    nc.sync.dma_start(out=out_rows[:, rows, cols], in_=y[:, rows, :])
                if last and t % 2:
                    weave(nc.vector.tensor_copy, y_bf[:, :, t - 1 : t + 1], y[:, t - 1 : t + 1, :])
            if not last:
                weave(nc.vector.tensor_copy, y_bf[:], y[:])
            quantize(nc, y_codes[:, cols], y_scales[:, cols], y_bf[:])
            if c >= 2:
                done = slice(0, j0 + w) if c == 2 else cols
                nc.sync.dma_start(out=out_words[:, done], in_=y_codes[:, done].bitcast(I32))
        for q in range(4):
            queue = nc.scalar if q % 2 else nc.sync
            queue.dma_start(
                out=out_2[0, 4 * q : 4 * q + 4, :].bitcast(I32),
                in_=y_scales[32 * q : 32 * q + 4, :].bitcast(I32),
            )
